import numpy as np
import ml_dtypes


def mxq(x, axis, fmt="e4m3"):
    dtype, down = {"e4m3": (ml_dtypes.float8_e4m3fn, 7), "e5m2": (ml_dtypes.float8_e5m2, 14)}[fmt]
    v = np.moveaxis(np.asarray(x, np.float32).astype(ml_dtypes.bfloat16).astype(np.float64), axis, -1)
    blocks = v.reshape(v.shape[:-1] + (-1, 32))
    amax = np.abs(blocks).max(-1, keepdims=True)
    byte = np.maximum(np.where(amax > 0, np.frexp(amax)[1] - 1 + 127, 0) - down, 1)
    scale = np.exp2(byte - 127.0)
    codes = (blocks / scale).astype(np.float32).astype(dtype).astype(np.float64)
    return np.moveaxis((codes * scale).reshape(v.shape), -1, axis)


WIDE = False


def mx_kscale(k):
    if not WIDE:
        return np.ones(k)
    levels = np.array([10, -10, 5, -5, 0])
    if k % 512:
        return np.exp2(np.random.permutation(np.resize(levels, k // 32))).repeat(32)
    a = np.empty((k // 512, 16))
    for p in range(k // 512):
        a[p, :8] = np.random.permutation(np.resize(levels, 8))
        for g in range(8):
            far = levels[np.abs(levels - a[p, g]) >= 10]
            a[p, g + 8] = far[np.random.randint(len(far))]
    return np.exp2(a.ravel()).repeat(32)


def f64(x):
    return np.asarray(x).astype(np.float64)


def striped(idx):
    return np.tile(np.asarray(idx).reshape(-1, 16).T, (8, 1)).astype(np.uint16)


def unstriped(offs):
    return offs[:16].T.reshape(-1).astype(np.int64)


E2M1 = np.array([0.0, 0.5, 1.0, 1.5, 2.0, 3.0, 4.0, 6.0, -0.0, -0.5, -1.0, -1.5, -2.0, -3.0, -4.0, -6.0])


def pack_weight(w, fmt):
    k, n = w.shape
    w = f64(np.asarray(w, np.float32).astype(ml_dtypes.bfloat16)).reshape(k // 32, 32, n)
    amax = np.abs(w).max(1)
    if fmt == "e4m3":
        byte = np.frexp(amax)[1] - 1 + 127 - 7
    else:
        mant, ex = np.frexp(amax / 6.0)
        byte = np.where(mant > 0.5, ex, ex - 1) + 127
    byte = np.clip(np.where(amax > 0, byte, 1), 1, 254)
    scaled = (w * np.exp2(127.0 - byte)[:, None, :]).reshape(k, n).astype(np.float32)
    by_word = np.ascontiguousarray(scaled.reshape(k // 512, 128, 4, n).transpose(0, 1, 3, 2))
    if fmt == "e4m3":
        words = by_word.astype(ml_dtypes.float8_e4m3fn).view(np.uint8)
    else:
        c = by_word.astype(ml_dtypes.float4_e2m1fn).view(np.uint8) & 0xF
        words = (c[..., 0::2] | (c[..., 1::2] << 4)).reshape(k // 512, 128, 2 * n)
    return np.ascontiguousarray(words), np.ascontiguousarray(byte.astype(np.uint8).reshape(k // 512, 16, n))


def unpack_weight(words, scales, fmt):
    g, _, n = scales.shape
    words = np.ascontiguousarray(words).reshape(g, 128, n, -1)
    if fmt == "e4m3":
        vals = words.view(ml_dtypes.float8_e4m3fn).astype(np.float64)
    else:
        nib = np.empty((g, 128, n, 4), np.uint8)
        nib[..., 0::2] = words & 0xF
        nib[..., 1::2] = words >> 4
        vals = E2M1[nib]
    vals = vals * np.repeat(np.exp2(scales.astype(np.float64) - 127.0), 8, axis=1)[..., None]
    return vals.transpose(0, 1, 3, 2).reshape(g * 512, n)


B, N, T, D, DV, NQ = 1, 1024, 2048, 512, 256, 256
CAP = 2.0


def setup_inputs():
    n = np.random.standard_normal
    idx = np.sort(np.random.permutation(T)[:B * N].reshape(B, N), axis=1).reshape(-1)
    s = mx_kscale(D)[:, None]
    u = np.ones(T)
    u[idx] = mx_kscale(B * N)
    r = np.random.uniform(0.5, 2.0, T)
    k = n((D, T)) / s
    v = n((DV, T)) / (u * r)
    kp = pack_weight(k, "e4m3")
    return {
        "qT": (n((B, D, NQ)) * s * (0.80 / np.sqrt(D))).astype(np.float32),
        "k_words": kp[0],
        "k_scales": kp[1],
        "vT": v.astype(np.float32),
        "vs": np.tile(u * r, (128, 1)).astype(np.float32),
        "kb": np.tile(n(T), (128, 1)).astype(np.float32),
        "offs": striped(idx),
    }


def reference(qT, k_words, k_scales, vT, vs, kb, offs):
    idx = unstriped(offs)
    k = unpack_weight(k_words, k_scales, "e4m3")
    v = f64(vT)
    pick = lambda x: x[:, idx].reshape(x.shape[0], B, N).transpose(1, 0, 2)
    q = f64(qT)
    score = mxq(q, 1, "e4m3").transpose(0, 2, 1) @ pick(k)
    score = score + pick(f64(kb))[:, :1, :]
    score = CAP * np.tanh(score / CAP)
    m = score.max(-1, keepdims=True)
    p = np.exp(score - m)
    total = p.sum(-1, keepdims=True)
    w = p * pick(f64(vs))[:, :1, :]
    y = mxq(w, 2, "e4m3") @ mxq(pick(v).transpose(0, 2, 1), 1, "e4m3")
    y = y / total
    return y

@@ -1,0 +1,244 @@
+from contextlib import ExitStack
+
+import concourse.mybir as mybir
+from concourse.masks import make_identity
+
+N, T, D, DV, NQ = 1024, 2048, 512, 256, 256
+CAP = 2.0
+FLOPS = 2 * NQ * N * (D + DV)
+
+F32 = mybir.dt.float32
+BF16 = mybir.dt.bfloat16
+I32 = mybir.dt.int32
+U32 = mybir.dt.uint32
+U16 = mybir.dt.uint16
+U8 = mybir.dt.uint8
+FP8X4 = mybir.dt.float8_e4m3fn_x4
+ACT = mybir.ActivationFunctionType
+ALU = mybir.AluOpType
+AXIS = mybir.AxisListType
+
+P = 128
+PACK = 4
+PASS = P * PACK
+PASSES = N // PASS
+QBLOCKS = NQ // P
+VBLOCKS = DV // P
+LIVE = P - 1
+LIST_COLS = PASS // 16
+
+
+def tile_attend_soft_cap_kb_srtq256n1024t2048_kernel(tc, qT, k_words, k_scales, vT, vs, kb, offs, out):
+    nc = tc.nc
+    with ExitStack() as ctx:
+        keep = ctx.enter_context(tc.tile_pool(name="keep", bufs=1))
+        psum = ctx.enter_context(tc.psum_pool(name="psum", bufs=1))
+        banks = [psum.tile([P, PASS], F32, name="bank%d" % b) for b in range(8)]
+
+        def sb(shape, dtype, name, slot=""):
+            return keep.tile(shape, dtype, name=name, tag=slot or name, align_bytes=64)
+
+        offsets = keep.tile([P, N // 16], U16, name="offsets")
+        ks_pool = sb([P, T], U8, "ks_pool")
+        kb_pool = sb([P, T], F32, "kb_pool")
+        vs_pool = sb([P, T], F32, "vs_pool")
+        kw_pool = sb([P, T], U32, "kw_pool")
+        v_pool = [sb([P, T], F32, "v_pool%d" % h) for h in range(VBLOCKS)]
+        q_raw = sb([P, PACK, NQ], F32, "q_raw")
+        ident = sb([P, P], F32, "ident")
+
+        make_identity(nc, ident[:])
+        nc.vector.memset(kb_pool[0:LIVE, :], 0.0)
+        nc.gpsimd.memset(vs_pool[0:LIVE, :], 0.0)
+
+        nc.sync.dma_start(offsets[:], offs)
+        nc.sync.dma_start(kb_pool[LIVE:P, :], kb[0:1, :])
+        for quad in range(4):
+            nc.sync.dma_start(
+                ks_pool[32 * quad : 32 * (quad + 1), :].bitcast(I32),
+                k_scales[0, 4 * quad : 4 * quad + 4, :].bitcast(I32).partition_broadcast(8),
+            )
+        nc.sync.dma_start(vs_pool[LIVE:P, :], vs[0:1, :])
+        nc.sync.dma_start(q_raw[:], qT[0].rearrange("(p j) q -> p j q", j=PACK))
+        nc.sync.dma_start(kw_pool[:].bitcast(I32), k_words[0].rearrange("p t r -> p (t r)").bitcast(I32))
+        for h in range(VBLOCKS):
+            nc.sync.dma_start(v_pool[h][:], vT[P * h : P * (h + 1), :])
+
+        def listed(g):
+            return offsets[:, LIST_COLS * g : LIST_COLS * (g + 1)]
+
+        kb_row = sb([P, N], F32, "kb_row")
+        nc.scalar.activation(kb_row[:], kb_pool[:].indirect(offsets[:]), ACT.Copy)
+        ks_g = sb([P, N], U8, "ks_g")
+        nc.vector.tensor_copy(ks_g[:], ks_pool[:].indirect(offsets[:]))
+        vs_row = sb([P, N], F32, "vs_row")
+        nc.scalar.activation(vs_row[:], vs_pool[:].indirect(offsets[:]), ACT.Copy)
+
+        kw_g = [sb([P, PASS], U32, "kw_g%d" % g) for g in range(PASSES)]
+        q_bf = sb([P, NQ, PACK], BF16, "q_bf")
+        nc.vector.tensor_copy(q_bf[:], q_raw[:].rearrange("p j q -> p q j"))
+        q_codes = sb([P, NQ], U32, "q_codes")
+        q_sc = sb([P, NQ], U8, "q_sc")
+        nc.vector.quantize_mx(q_codes[:].bitcast(FP8X4), q_sc[:], q_bf[:].rearrange("p q j -> p (q j)"))
+
+        kb_col = [sb([P, PACK], F32, "kb_col%d" % g) for g in range(PASSES)]
+        for g in range(PASSES):
+            bank = banks[g]
+            for j in range(PACK):
+                nc.tensor.transpose(bank[:, P * j : P * (j + 1)], kb_row[:, PASS * g + P * j : PASS * g + P * (j + 1)], ident[:])
+            nc.scalar.activation(kb_col[g][:], bank[:, LIVE:PASS:P], ACT.Copy, scale=1.0 / CAP)
+
+        for g in range(PASSES):
+            nc.vector.tensor_copy(kw_g[g][:], kw_pool[:].indirect(listed(g)))
+
+        th = [sb([P, NQ], F32, "th%d" % j) for j in range(N // P)]
+        tmax = [sb([P, PASSES], F32, "tmax%d" % b) for b in range(QBLOCKS)]
+        v_g = {}
+        vs_col = [sb([P, PACK], F32, "vs_col%d" % g) for g in range(PASSES)]
+
+        def capped_bank(b, g):
+            return banks[QBLOCKS * g + b]
+
+        def scores(g):
+            for j in range(PACK):
+                bank = banks[4 + 2 * g + j // 2]
+                cols = slice(NQ * (j % 2), NQ * (j % 2 + 1))
+                nc.tensor.matmul_mx(
+                    out=bank[:, cols],
+                    lhsT=kw_g[g][:, P * j : P * (j + 1)].bitcast(FP8X4),
+                    lhsT_scale=ks_g[:, PASS * g + P * j : PASS * g + P * (j + 1)],
+                    rhs=q_codes[:].bitcast(FP8X4),
+                    rhs_scale=q_sc[:],
+                    start=True,
+                    stop=True,
+                )
+
+        def cap(g):
+            for j in range(PACK):
+                bank = banks[4 + 2 * g + j // 2]
+                cols = slice(NQ * (j % 2), NQ * (j % 2 + 1))
+                nc.scalar.activation(th[PACK * g + j][:], bank[:, cols], ACT.Tanh, bias=kb_col[g][:, j : j + 1], scale=1.0 / CAP)
+
+        def turn_capped(g):
+            for b in range(QBLOCKS):
+                for j in range(PACK):
+                    nc.tensor.transpose(capped_bank(b, g)[:, P * j : P * (j + 1)], th[PACK * g + j][:, P * b : P * (b + 1)], ident[:])
+
+        def row_max(g):
+            for b in range(QBLOCKS):
+                nc.vector.tensor_reduce(tmax[b][:, g : g + 1], capped_bank(b, g)[:], AXIS.X, ALU.max)
+
+        scores(0)
+        cap(0)
+        scores(1)
+        turn_capped(0)
+        cap(1)
+        v_g[0, 0] = sb([P, PASS], BF16, "v_g00")
+        nc.vector.tensor_copy(v_g[0, 0][:], v_pool[0][:].indirect(listed(0)))
+        row_max(0)
+        turn_capped(1)
+        row_max(1)
+
+        for g in range(PASSES):
+            bank = banks[4 + g]
+            for r in range(PACK):
+                nc.tensor.transpose(bank[:, P * r : P * (r + 1)], vs_row[:, PASS * g + r : PASS * (g + 1) : PACK], ident[:])
+            nc.scalar.copy(vs_col[g][:], bank[:, LIVE:PASS:P])
+
+        neg_m = [sb([P, 1], F32, "neg_m%d" % b) for b in range(QBLOCKS)]
+        for b in range(QBLOCKS):
+            nc.vector.tensor_scalar(neg_m[b][:], tmax[b][:, 0:1], tmax[b][:, 1:2], -CAP, ALU.max, ALU.mult)
+
+        v_g[1, 0] = sb([P, PASS], BF16, "v_g10", slot="kb_col1")
+        nc.scalar.activation(v_g[1, 0][:], v_pool[1][:].indirect(listed(0)), ACT.Copy)
+        v_g[0, 1] = sb([P, PASS], BF16, "v_g01", slot="tmax1")
+        nc.vector.tensor_copy(v_g[0, 1][:], v_pool[0][:].indirect(listed(1)))
+
+        part = [sb([P, PASSES], F32, "part%d" % b) for b in range(QBLOCKS)]
+        p_sb = {}
+        w_codes = {}
+        w_sc = {}
+        for b in range(QBLOCKS):
+            for g in range(PASSES):
+                p_sb[b, g] = sb([P, PACK, P], F32, "p%d%d" % (b, g))
+                nc.scalar.activation(
+                    p_sb[b, g][:],
+                    capped_bank(b, g)[:].rearrange("q (s r) -> q r s", r=PACK),
+                    ACT.Exp,
+                    bias=neg_m[b][:],
+                    scale=CAP,
+                    accum_out=part[b][:, g : g + 1],
+                )
+
+        v_g[1, 1] = sb([P, PASS], BF16, "v_g11", slot="neg_m1")
+        nc.scalar.activation(v_g[1, 1][:], v_pool[1][:].indirect(listed(1)), ACT.Copy)
+
+        v_codes = [sb([P, DV], U32, "v_codes%d" % g) for g in range(PASSES)]
+        v_sc = [sb([P, DV], U8, "v_sc%d" % g) for g in range(PASSES)]
+        v_bf = [sb([P, DV, PACK], BF16, "v_bf%d" % g) for g in range(PASSES)]
+        w_bf = {}
+
+        def turn_values(g):
+            bank = banks[4 + g]
+            for h in range(VBLOCKS):
+                pairs = v_g[h, g][:].bitcast(F32)
+                for u in range(2):
+                    at = P * (2 * h + u)
+                    nc.tensor.transpose(bank[:, at : at + P], pairs[:, u : 2 * P : 2], ident[:])
+            nc.scalar.copy(
+                v_bf[g][:].rearrange("s e r -> s (e r)").bitcast(F32).rearrange("s (h f u) -> s h f u", h=VBLOCKS, u=2),
+                bank[:].rearrange("s (h u f) -> s h f u", h=VBLOCKS, u=2),
+            )
+
+        def weights(b, g):
+            bank = banks[6 + g] if b == 0 else capped_bank(0, g)
+            for r in range(PACK):
+                nc.tensor.transpose(bank[:, P * r : P * (r + 1)], p_sb[b, g][:, r, :], ident[:])
+            w_bf[b, g] = sb([P, P, PACK], BF16, "w_bf%d%d" % (b, g))
+            nc.vector.tensor_tensor(
+                w_bf[b, g][:],
+                bank[:].rearrange("s (r q) -> s q r", r=PACK),
+                vs_col[g][:].unsqueeze(1).to_broadcast([P, P, PACK]),
+                ALU.mult,
+            )
+
+        def quantise_weights(b, g):
+            w_codes[b, g] = sb([P, P], U32, "w_codes%d%d" % (b, g))
+            w_sc[b, g] = sb([P, P], U8, "w_sc%d%d" % (b, g))
+            nc.vector.quantize_mx(w_codes[b, g][:].bitcast(FP8X4), w_sc[b, g][:], w_bf[b, g][:].rearrange("s q r -> s (q r)"))
+
+        def quantise_values(g):
+            nc.vector.quantize_mx(v_codes[g][:].bitcast(FP8X4), v_sc[g][:], v_bf[g][:].rearrange("s e r -> s (e r)"))
+
+        weights(0, 0)
+        weights(0, 1)
+        quantise_weights(0, 0)
+        turn_values(0)
+        weights(1, 0)
+        quantise_weights(0, 1)
+        turn_values(1)
+        weights(1, 1)
+        quantise_values(0)
+        quantise_weights(1, 0)
+        quantise_values(1)
+        quantise_weights(1, 1)
+
+        for b in range(QBLOCKS):
+            total = sb([P, 1], F32, "total%d" % b)
+            nc.vector.tensor_tensor(total[:], part[b][:, 0:1], part[b][:, 1:2], ALU.add)
+            inv = sb([P, 1], F32, "inv%d" % b)
+            nc.vector.reciprocal(inv[:], total[:])
+            bank = banks[6 + b]
+            for g in range(PASSES):
+                nc.tensor.matmul_mx(
+                    out=bank[:, 0:DV],
+                    lhsT=w_codes[b, g][:].bitcast(FP8X4),
+                    lhsT_scale=w_sc[b, g][:],
+                    rhs=v_codes[g][:].bitcast(FP8X4),
+                    rhs_scale=v_sc[g][:],
+                    start=(g == 0),
+                    stop=(g == PASSES - 1),
+                )
+            y = sb([P, DV], F32, "y%d" % b)
+            nc.scalar.activation(y[:], bank[:, 0:DV], ACT.Copy, scale=inv[:])
+            nc.sync.dma_start(out[0, P * b : P * (b + 1), :], y[:])

@@ -47,18 +47,25 @@ def tile_attend_soft_cap_kb_srtq256n1024t2048_kernel(tc, qT, k_words, k_scales, 
         q_raw = sb([P, PACK, NQ], F32, "q_raw")
         ident = sb([P, P], F32, "ident")
 
+        ks_words = ks_pool[:].bitcast(I32)
+        nc.vector.memset(ks_words[:, 0 : T // 8], 0)
+        nc.gpsimd.memset(ks_words[:, T // 8 : T // 4], 0)
+        seed = sb([P, 1], F32, "seed")
+        nc.vector.memset(seed[:], 0.0)
         make_identity(nc, ident[:])
-        nc.vector.memset(kb_pool[0:LIVE, :], 0.0)
-        nc.gpsimd.memset(vs_pool[0:LIVE, :], 0.0)
+        nc.vector.memset(kb_pool[0:LIVE, :].bitcast(I32), 0)
+        nc.vector.memset(vs_pool[0:LIVE, :].bitcast(I32), 0)
+        warm = sb([P, 1], F32, "warm")
+        nc.scalar.activation(warm[:], seed[:], ACT.Tanh, bias=seed[:])
 
         nc.sync.dma_start(offsets[:], offs)
         nc.sync.dma_start(kb_pool[LIVE:P, :], kb[0:1, :])
+        nc.sync.dma_start(vs_pool[LIVE:P, :], vs[0:1, :])
         for quad in range(4):
             nc.sync.dma_start(
-                ks_pool[32 * quad : 32 * (quad + 1), :].bitcast(I32),
-                k_scales[0, 4 * quad : 4 * quad + 4, :].bitcast(I32).partition_broadcast(8),
+                ks_pool[32 * quad : 32 * quad + 4, :].bitcast(I32),
+                k_scales[0, 4 * quad : 4 * quad + 4, :].bitcast(I32),
             )
-        nc.sync.dma_start(vs_pool[LIVE:P, :], vs[0:1, :])
         nc.sync.dma_start(q_raw[:], qT[0].rearrange("(p j) q -> p j q", j=PACK))
         nc.sync.dma_start(kw_pool[:].bitcast(I32), k_words[0].rearrange("p t r -> p (t r)").bitcast(I32))
         for h in range(VBLOCKS):
@@ -69,35 +76,37 @@ def tile_attend_soft_cap_kb_srtq256n1024t2048_kernel(tc, qT, k_words, k_scales, 
 
         kb_row = sb([P, N], F32, "kb_row")
         nc.scalar.activation(kb_row[:], kb_pool[:].indirect(offsets[:]), ACT.Copy)
+        kw_g = [sb([P, 2 * P], U32, "kw_g%d" % c) for c in range(2 * PASSES)]
+        q_bf = sb([P, NQ, PACK], BF16, "q_bf")
+        nc.scalar.copy(q_bf[:], q_raw[:].rearrange("p j q -> p q j"))
+        vs_row = sb([P, N], F32, "vs_row", slot="q_raw")
+        nc.scalar.activation(vs_row[:], vs_pool[:].indirect(offsets[:]), ACT.Copy)
         ks_g = sb([P, N], U8, "ks_g")
         nc.vector.tensor_copy(ks_g[:], ks_pool[:].indirect(offsets[:]))
-        vs_row = sb([P, N], F32, "vs_row")
-        nc.scalar.activation(vs_row[:], vs_pool[:].indirect(offsets[:]), ACT.Copy)
-
-        kw_g = [sb([P, PASS], U32, "kw_g%d" % g) for g in range(PASSES)]
-        q_bf = sb([P, NQ, PACK], BF16, "q_bf")
-        nc.vector.tensor_copy(q_bf[:], q_raw[:].rearrange("p j q -> p q j"))
         q_codes = sb([P, NQ], U32, "q_codes")
         q_sc = sb([P, NQ], U8, "q_sc")
         nc.vector.quantize_mx(q_codes[:].bitcast(FP8X4), q_sc[:], q_bf[:].rearrange("p q j -> p (q j)"))
 
-        kb_col = [sb([P, PACK], F32, "kb_col%d" % g) for g in range(PASSES)]
+        kb_col = sb([P, PASSES, PACK], F32, "kb_col", slot="vs_pool")
         for g in range(PASSES):
             bank = banks[g]
             for j in range(PACK):
                 nc.tensor.transpose(bank[:, P * j : P * (j + 1)], kb_row[:, PASS * g + P * j : PASS * g + P * (j + 1)], ident[:])
-            nc.scalar.activation(kb_col[g][:], bank[:, LIVE:PASS:P], ACT.Copy, scale=1.0 / CAP)
+            nc.scalar.activation(kb_col[:, g, :], bank[:, LIVE:PASS:P], ACT.Copy, scale=1.0 / CAP)
 
-        for g in range(PASSES):
-            nc.vector.tensor_copy(kw_g[g][:], kw_pool[:].indirect(listed(g)))
+        for c in range(2 * PASSES):
+            nc.vector.tensor_copy(kw_g[c][:], kw_pool[:].indirect(offsets[:, 16 * c : 16 * (c + 1)]))
 
         th = [sb([P, NQ], F32, "th%d" % j) for j in range(N // P)]
-        tmax = [sb([P, PASSES], F32, "tmax%d" % b) for b in range(QBLOCKS)]
+        neg_c = {}
+        neg_max = {}
         v_g = {}
         vs_col = [sb([P, PACK], F32, "vs_col%d" % g) for g in range(PASSES)]
+        for g in range(PASSES):
+            nc.sync.dma_start(vs_col[g][:], vs_row[LIVE:P, PASS * g : PASS * (g + 1)].rearrange("o (s r) -> o s r", r=PACK))
 
         def capped_bank(b, g):
-            return banks[QBLOCKS * g + b]
+            return banks[((0, 1), (7, 0))[b][g]]
 
         def scores(g):
             for j in range(PACK):
@@ -105,7 +114,7 @@ def tile_attend_soft_cap_kb_srtq256n1024t2048_kernel(tc, qT, k_words, k_scales, 
                 cols = slice(NQ * (j % 2), NQ * (j % 2 + 1))
                 nc.tensor.matmul_mx(
                     out=bank[:, cols],
-                    lhsT=kw_g[g][:, P * j : P * (j + 1)].bitcast(FP8X4),
+                    lhsT=kw_g[2 * g + j // 2][:, P * (j % 2) : P * (j % 2 + 1)].bitcast(FP8X4),
                     lhsT_scale=ks_g[:, PASS * g + P * j : PASS * g + P * (j + 1)],
                     rhs=q_codes[:].bitcast(FP8X4),
                     rhs_scale=q_sc[:],
@@ -117,42 +126,47 @@ def tile_attend_soft_cap_kb_srtq256n1024t2048_kernel(tc, qT, k_words, k_scales, 
             for j in range(PACK):
                 bank = banks[4 + 2 * g + j // 2]
                 cols = slice(NQ * (j % 2), NQ * (j % 2 + 1))
-                nc.scalar.activation(th[PACK * g + j][:], bank[:, cols], ACT.Tanh, bias=kb_col[g][:, j : j + 1], scale=1.0 / CAP)
+                nc.scalar.activation(th[PACK * g + j][:], bank[:, cols], ACT.Tanh, bias=kb_col[:, g, j : j + 1], scale=1.0 / CAP)
 
-        def turn_capped(g):
-            for b in range(QBLOCKS):
+        def turn_capped(b, g):
+            if True:
                 for j in range(PACK):
                     nc.tensor.transpose(capped_bank(b, g)[:, P * j : P * (j + 1)], th[PACK * g + j][:, P * b : P * (b + 1)], ident[:])
 
-        def row_max(g):
-            for b in range(QBLOCKS):
-                nc.vector.tensor_reduce(tmax[b][:, g : g + 1], capped_bank(b, g)[:], AXIS.X, ALU.max)
+        def row_max(b, g):
+            if True:
+                neg_c[b, g] = sb([P, PACK, P], F32, "neg_c%d%d" % (b, g))
+                neg_max[b, g] = sb([P, 1], F32, "neg_max%d%d" % (b, g))
+                nc.vector.tensor_scalar(
+                    neg_c[b, g][:],
+                    capped_bank(b, g)[:].rearrange("q (s r) -> q r s", r=PACK),
+                    -CAP,
+                    neg_max[b, g - 1][:] if g > 0 else None,
+                    ALU.mult,
+                    ALU.min,
+                    accum_out=neg_max[b, g][:],
+                )
 
         scores(0)
-        cap(0)
         scores(1)
-        turn_capped(0)
+        cap(0)
         cap(1)
         v_g[0, 0] = sb([P, PASS], BF16, "v_g00")
         nc.vector.tensor_copy(v_g[0, 0][:], v_pool[0][:].indirect(listed(0)))
-        row_max(0)
-        turn_capped(1)
-        row_max(1)
-
-        for g in range(PASSES):
-            bank = banks[4 + g]
-            for r in range(PACK):
-                nc.tensor.transpose(bank[:, P * r : P * (r + 1)], vs_row[:, PASS * g + r : PASS * (g + 1) : PACK], ident[:])
-            nc.scalar.copy(vs_col[g][:], bank[:, LIVE:PASS:P])
-
-        neg_m = [sb([P, 1], F32, "neg_m%d" % b) for b in range(QBLOCKS)]
-        for b in range(QBLOCKS):
-            nc.vector.tensor_scalar(neg_m[b][:], tmax[b][:, 0:1], tmax[b][:, 1:2], -CAP, ALU.max, ALU.mult)
-
-        v_g[1, 0] = sb([P, PASS], BF16, "v_g10", slot="kb_col1")
-        nc.scalar.activation(v_g[1, 0][:], v_pool[1][:].indirect(listed(0)), ACT.Copy)
-        v_g[0, 1] = sb([P, PASS], BF16, "v_g01", slot="tmax1")
+        v_g[0, 1] = sb([P, PASS], BF16, "v_g01")
         nc.vector.tensor_copy(v_g[0, 1][:], v_pool[0][:].indirect(listed(1)))
+        turn_capped(0, 0)
+        turn_capped(0, 1)
+        row_max(0, 0)
+        row_max(0, 1)
+        turn_capped(1, 0)
+        turn_capped(1, 1)
+        row_max(1, 0)
+        row_max(1, 1)
+        v_g[1, 0] = sb([P, PASS], BF16, "v_g10", slot="vs_pool")
+        nc.scalar.activation(v_g[1, 0][:], v_pool[1][:].indirect(listed(0)), ACT.Copy)
+        v_g[1, 1] = sb([P, PASS], BF16, "v_g11", slot="neg_max10")
+        nc.vector.tensor_copy(v_g[1, 1][:, 0 : PASS // 2], v_pool[1][:].indirect(offsets[:, 32:48]))
 
         part = [sb([P, PASSES], F32, "part%d" % b) for b in range(QBLOCKS)]
         p_sb = {}
@@ -163,35 +177,37 @@ def tile_attend_soft_cap_kb_srtq256n1024t2048_kernel(tc, qT, k_words, k_scales, 
                 p_sb[b, g] = sb([P, PACK, P], F32, "p%d%d" % (b, g))
                 nc.scalar.activation(
                     p_sb[b, g][:],
-                    capped_bank(b, g)[:].rearrange("q (s r) -> q r s", r=PACK),
+                    neg_c[b, g][:],
                     ACT.Exp,
-                    bias=neg_m[b][:],
-                    scale=CAP,
+                    bias=neg_max[b, PASSES - 1][:],
+                    scale=-1.0,
                     accum_out=part[b][:, g : g + 1],
                 )
 
-        v_g[1, 1] = sb([P, PASS], BF16, "v_g11", slot="neg_m1")
-        nc.scalar.activation(v_g[1, 1][:], v_pool[1][:].indirect(listed(1)), ACT.Copy)
+        nc.scalar.activation(v_g[1, 1][:, PASS // 2 : PASS], v_pool[1][:].indirect(offsets[:, 48:64]), ACT.Copy)
 
         v_codes = [sb([P, DV], U32, "v_codes%d" % g) for g in range(PASSES)]
         v_sc = [sb([P, DV], U8, "v_sc%d" % g) for g in range(PASSES)]
-        v_bf = [sb([P, DV, PACK], BF16, "v_bf%d" % g) for g in range(PASSES)]
+        v_bf = [sb([P, DV, PACK], BF16, "v_bf0", slot="neg_max11"), sb([P, DV, PACK], BF16, "v_bf1")]
         w_bf = {}
 
         def turn_values(g):
-            bank = banks[4 + g]
+            bank = banks[(1, 2)[g]]
             for h in range(VBLOCKS):
                 pairs = v_g[h, g][:].bitcast(F32)
                 for u in range(2):
                     at = P * (2 * h + u)
                     nc.tensor.transpose(bank[:, at : at + P], pairs[:, u : 2 * P : 2], ident[:])
+
+        def lay_values(g):
+            bank = banks[(1, 2)[g]]
             nc.scalar.copy(
                 v_bf[g][:].rearrange("s e r -> s (e r)").bitcast(F32).rearrange("s (h f u) -> s h f u", h=VBLOCKS, u=2),
                 bank[:].rearrange("s (h u f) -> s h f u", h=VBLOCKS, u=2),
             )
 
         def weights(b, g):
-            bank = banks[6 + g] if b == 0 else capped_bank(0, g)
+            bank = banks[2 + 2 * b + g]
             for r in range(PACK):
                 nc.tensor.transpose(bank[:, P * r : P * (r + 1)], p_sb[b, g][:, r, :], ident[:])
             w_bf[b, g] = sb([P, P, PACK], BF16, "w_bf%d%d" % (b, g))
@@ -210,28 +226,31 @@ def tile_attend_soft_cap_kb_srtq256n1024t2048_kernel(tc, qT, k_words, k_scales, 
         def quantise_values(g):
             nc.vector.quantize_mx(v_codes[g][:].bitcast(FP8X4), v_sc[g][:], v_bf[g][:].rearrange("s e r -> s (e r)"))
 
+        turn_values(0)
         weights(0, 0)
         weights(0, 1)
         quantise_weights(0, 0)
-        turn_values(0)
         weights(1, 0)
         quantise_weights(0, 1)
+        lay_values(0)
         turn_values(1)
+        lay_values(1)
         weights(1, 1)
         quantise_values(0)
         quantise_weights(1, 0)
         quantise_values(1)
         quantise_weights(1, 1)
-
+        inv = []
         for b in range(QBLOCKS):
             total = sb([P, 1], F32, "total%d" % b)
-            nc.vector.tensor_tensor(total[:], part[b][:, 0:1], part[b][:, 1:2], ALU.add)
-            inv = sb([P, 1], F32, "inv%d" % b)
-            nc.vector.reciprocal(inv[:], total[:])
-            bank = banks[6 + b]
-            for g in range(PASSES):
+            nc.gpsimd.tensor_tensor(total[:], part[b][:, 0:1], part[b][:, 1:2], ALU.add)
+            inv.append(sb([P, 1], F32, "inv%d" % b))
+            nc.vector.reciprocal(inv[b][:], total[:])
+
+        for g in range(PASSES):
+            for b in range(QBLOCKS):
                 nc.tensor.matmul_mx(
-                    out=bank[:, 0:DV],
+                    out=banks[6 + b][:, 0:DV],
                     lhsT=w_codes[b, g][:].bitcast(FP8X4),
                     lhsT_scale=w_sc[b, g][:],
                     rhs=v_codes[g][:].bitcast(FP8X4),
@@ -239,6 +258,8 @@ def tile_attend_soft_cap_kb_srtq256n1024t2048_kernel(tc, qT, k_words, k_scales, 
                     start=(g == 0),
                     stop=(g == PASSES - 1),
                 )
-            y = sb([P, DV], F32, "y%d" % b)
-            nc.scalar.activation(y[:], bank[:, 0:DV], ACT.Copy, scale=inv[:])
-            nc.sync.dma_start(out[0, P * b : P * (b + 1), :], y[:])
+        y = [sb([P, DV], F32, "y%d" % b) for b in range(QBLOCKS)]
+        nc.scalar.activation(y[0][:], banks[6][:, 0:DV], ACT.Copy, scale=inv[0][:])
+        nc.vector.tensor_scalar(y[1][:], banks[7][:, 0:DV], inv[1][:], None, ALU.mult)
+        nc.scalar.dma_start(out[0, 0:P, :], y[0][:])
+        nc.sync.dma_start(out[0, P : 2 * P, :], y[1][:])

@@ -16,7 +16,6 @@ U8 = mybir.dt.uint8
 FP8X4 = mybir.dt.float8_e4m3fn_x4
 ACT = mybir.ActivationFunctionType
 ALU = mybir.AluOpType
-AXIS = mybir.AxisListType
 
 P = 128
 PACK = 4
@@ -25,7 +24,8 @@ PASSES = N // PASS
 QBLOCKS = NQ // P
 VBLOCKS = DV // P
 LIVE = P - 1
-LIST_COLS = PASS // 16
+QUARTER = N // 4
+EARLY = T - N + PASS
 
 
 def tile_attend_soft_cap_kb_srtq256n1024t2048_kernel(tc, qT, k_words, k_scales, vT, vs, kb, offs, out):
@@ -33,12 +33,16 @@ def tile_attend_soft_cap_kb_srtq256n1024t2048_kernel(tc, qT, k_words, k_scales, 
     with ExitStack() as ctx:
         keep = ctx.enter_context(tc.tile_pool(name="keep", bufs=1))
         psum = ctx.enter_context(tc.psum_pool(name="psum", bufs=1))
-        banks = [psum.tile([P, PASS], F32, name="bank%d" % b) for b in range(8)]
+        banks = [psum.tile([P, PASS], F32, name="bank%d" % n) for n in range(8)]
 
-        def sb(shape, dtype, name, slot=""):
-            return keep.tile(shape, dtype, name=name, tag=slot or name, align_bytes=64)
+        def sb(shape, dtype, name, after=""):
+            return keep.tile(shape, dtype, name=name, tag=after or name, align_bytes=64)
 
         offsets = keep.tile([P, N // 16], U16, name="offsets")
+
+        def listed(first, last):
+            return offsets[:, first // 16 : last // 16]
+
         ks_pool = sb([P, T], U8, "ks_pool")
         kb_pool = sb([P, T], F32, "kb_pool")
         vs_pool = sb([P, T], F32, "vs_pool")
@@ -66,80 +70,80 @@ def tile_attend_soft_cap_kb_srtq256n1024t2048_kernel(tc, qT, k_words, k_scales, 
                 ks_pool[32 * quad : 32 * quad + 4, :].bitcast(I32),
                 k_scales[0, 4 * quad : 4 * quad + 4, :].bitcast(I32),
             )
-        nc.sync.dma_start(q_raw[:], qT[0].rearrange("(p j) q -> p j q", j=PACK))
+        nc.sync.dma_start(q_raw[:], qT[0].rearrange("(p r) q -> p r q", r=PACK))
         nc.sync.dma_start(kw_pool[:].bitcast(I32), k_words[0].rearrange("p t r -> p (t r)").bitcast(I32))
-        for h in range(VBLOCKS):
-            nc.sync.dma_start(v_pool[h][:], vT[P * h : P * (h + 1), :])
-
-        def listed(g):
-            return offsets[:, LIST_COLS * g : LIST_COLS * (g + 1)]
+        nc.sync.dma_start(v_pool[0][:], vT[0:P, :])
+        v_early = sb([P, EARLY], F32, "v_early")
+        nc.sync.dma_start(v_early[:], vT[P : 2 * P, 0:EARLY])
+        nc.sync.dma_start(v_pool[1][:], vT[P : 2 * P, :])
 
         kb_row = sb([P, N], F32, "kb_row")
         nc.scalar.activation(kb_row[:], kb_pool[:].indirect(offsets[:]), ACT.Copy)
-        kw_g = [sb([P, 2 * P], U32, "kw_g%d" % c) for c in range(2 * PASSES)]
+        key_words = [sb([P, QUARTER], U32, "key_words%d" % n) for n in range(N // QUARTER)]
         q_bf = sb([P, NQ, PACK], BF16, "q_bf")
-        nc.scalar.copy(q_bf[:], q_raw[:].rearrange("p j q -> p q j"))
-        vs_row = sb([P, N], F32, "vs_row", slot="q_raw")
+        nc.scalar.copy(q_bf[:], q_raw[:].rearrange("p r q -> p q r"))
+        vs_row = sb([P, N], F32, "vs_row", after="q_raw")
         nc.scalar.activation(vs_row[:], vs_pool[:].indirect(offsets[:]), ACT.Copy)
-        ks_g = sb([P, N], U8, "ks_g")
-        nc.vector.tensor_copy(ks_g[:], ks_pool[:].indirect(offsets[:]))
+        key_scales = sb([P, N], U8, "key_scales")
+        nc.vector.tensor_copy(key_scales[:], ks_pool[:].indirect(offsets[:]))
         q_codes = sb([P, NQ], U32, "q_codes")
-        q_sc = sb([P, NQ], U8, "q_sc")
-        nc.vector.quantize_mx(q_codes[:].bitcast(FP8X4), q_sc[:], q_bf[:].rearrange("p q j -> p (q j)"))
+        q_scales = sb([P, NQ], U8, "q_scales")
+        nc.vector.quantize_mx(q_codes[:].bitcast(FP8X4), q_scales[:], q_bf[:].rearrange("p q r -> p (q r)"))
 
-        kb_col = sb([P, PASSES, PACK], F32, "kb_col", slot="vs_pool")
+        half_bias = sb([P, PASSES, PACK], F32, "half_bias", after="vs_pool")
         for g in range(PASSES):
-            bank = banks[g]
             for j in range(PACK):
-                nc.tensor.transpose(bank[:, P * j : P * (j + 1)], kb_row[:, PASS * g + P * j : PASS * g + P * (j + 1)], ident[:])
-            nc.scalar.activation(kb_col[:, g, :], bank[:, LIVE:PASS:P], ACT.Copy, scale=1.0 / CAP)
+                first = PASS * g + P * j
+                nc.tensor.transpose(banks[g][:, P * j : P * (j + 1)], kb_row[:, first : first + P], ident[:])
+            nc.scalar.activation(half_bias[:, g, :], banks[g][:, LIVE:PASS:P], ACT.Copy, scale=1.0 / CAP)
 
-        for c in range(2 * PASSES):
-            nc.vector.tensor_copy(kw_g[c][:], kw_pool[:].indirect(offsets[:, 16 * c : 16 * (c + 1)]))
+        for n in range(N // QUARTER):
+            nc.vector.tensor_copy(key_words[n][:], kw_pool[:].indirect(listed(QUARTER * n, QUARTER * (n + 1))))
 
-        th = [sb([P, NQ], F32, "th%d" % j) for j in range(N // P)]
-        neg_c = {}
-        neg_max = {}
-        v_g = {}
         vs_col = [sb([P, PACK], F32, "vs_col%d" % g) for g in range(PASSES)]
         for g in range(PASSES):
             nc.sync.dma_start(vs_col[g][:], vs_row[LIVE:P, PASS * g : PASS * (g + 1)].rearrange("o (s r) -> o s r", r=PACK))
 
-        def capped_bank(b, g):
-            return banks[((0, 1), (7, 0))[b][g]]
+        def score_tile(g, j):
+            return banks[4 + 2 * g + j // 2][:, NQ * (j % 2) : NQ * (j % 2 + 1)]
 
-        def scores(g):
+        for g in range(PASSES):
             for j in range(PACK):
-                bank = banks[4 + 2 * g + j // 2]
-                cols = slice(NQ * (j % 2), NQ * (j % 2 + 1))
+                first = PASS * g + P * j
                 nc.tensor.matmul_mx(
-                    out=bank[:, cols],
-                    lhsT=kw_g[2 * g + j // 2][:, P * (j % 2) : P * (j % 2 + 1)].bitcast(FP8X4),
-                    lhsT_scale=ks_g[:, PASS * g + P * j : PASS * g + P * (j + 1)],
+                    out=score_tile(g, j),
+                    lhsT=key_words[first // QUARTER][:, first % QUARTER : first % QUARTER + P].bitcast(FP8X4),
+                    lhsT_scale=key_scales[:, first : first + P],
                     rhs=q_codes[:].bitcast(FP8X4),
-                    rhs_scale=q_sc[:],
+                    rhs_scale=q_scales[:],
                     start=True,
                     stop=True,
                 )
-
-        def cap(g):
+        tanh = {}
+        for g in range(PASSES):
             for j in range(PACK):
-                bank = banks[4 + 2 * g + j // 2]
-                cols = slice(NQ * (j % 2), NQ * (j % 2 + 1))
-                nc.scalar.activation(th[PACK * g + j][:], bank[:, cols], ACT.Tanh, bias=kb_col[:, g, j : j + 1], scale=1.0 / CAP)
+                tanh[g, j] = sb([P, NQ], F32, "tanh%d%d" % (g, j))
+                nc.scalar.activation(tanh[g, j][:], score_tile(g, j), ACT.Tanh, bias=half_bias[:, g, j : j + 1], scale=1.0 / CAP)
 
-        def turn_capped(b, g):
-            if True:
+        values = {}
+        for g in range(PASSES):
+            values[0, g] = sb([P, PASS], BF16, "values0%d" % g)
+            nc.vector.tensor_copy(values[0, g][:], v_pool[0][:].indirect(listed(PASS * g, PASS * (g + 1))))
+
+        capped_bank = {(0, 0): banks[0], (0, 1): banks[1], (1, 0): banks[7], (1, 1): banks[6]}
+        follows = {(0, 0): "v_pool0", (1, 0): "neg_max00"}
+        neg_c = {}
+        neg_max = {}
+        for b in range(QBLOCKS):
+            for g in range(PASSES):
                 for j in range(PACK):
-                    nc.tensor.transpose(capped_bank(b, g)[:, P * j : P * (j + 1)], th[PACK * g + j][:, P * b : P * (b + 1)], ident[:])
-
-        def row_max(b, g):
-            if True:
-                neg_c[b, g] = sb([P, PACK, P], F32, "neg_c%d%d" % (b, g))
+                    nc.tensor.transpose(capped_bank[b, g][:, P * j : P * (j + 1)], tanh[g, j][:, P * b : P * (b + 1)], ident[:])
+            for g in range(PASSES):
+                neg_c[b, g] = sb([P, PACK, P], F32, "neg_c%d%d" % (b, g), after=follows.get((b, g), ""))
                 neg_max[b, g] = sb([P, 1], F32, "neg_max%d%d" % (b, g))
                 nc.vector.tensor_scalar(
                     neg_c[b, g][:],
-                    capped_bank(b, g)[:].rearrange("q (s r) -> q r s", r=PACK),
+                    capped_bank[b, g][:].rearrange("q (s r) -> q r s", r=PACK),
                     -CAP,
                     neg_max[b, g - 1][:] if g > 0 else None,
                     ALU.mult,
@@ -147,119 +151,108 @@ def tile_attend_soft_cap_kb_srtq256n1024t2048_kernel(tc, qT, k_words, k_scales, 
                     accum_out=neg_max[b, g][:],
                 )
 
-        scores(0)
-        scores(1)
-        cap(0)
-        cap(1)
-        v_g[0, 0] = sb([P, PASS], BF16, "v_g00")
-        nc.vector.tensor_copy(v_g[0, 0][:], v_pool[0][:].indirect(listed(0)))
-        v_g[0, 1] = sb([P, PASS], BF16, "v_g01")
-        nc.vector.tensor_copy(v_g[0, 1][:], v_pool[0][:].indirect(listed(1)))
-        turn_capped(0, 0)
-        turn_capped(0, 1)
-        row_max(0, 0)
-        row_max(0, 1)
-        turn_capped(1, 0)
-        turn_capped(1, 1)
-        row_max(1, 0)
-        row_max(1, 1)
-        v_g[1, 0] = sb([P, PASS], BF16, "v_g10", slot="vs_pool")
-        nc.scalar.activation(v_g[1, 0][:], v_pool[1][:].indirect(listed(0)), ACT.Copy)
-        v_g[1, 1] = sb([P, PASS], BF16, "v_g11", slot="neg_max10")
-        nc.vector.tensor_copy(v_g[1, 1][:, 0 : PASS // 2], v_pool[1][:].indirect(offsets[:, 32:48]))
+        values[1, 0] = sb([P, PASS], BF16, "values10", after="vs_pool")
+        nc.scalar.activation(values[1, 0][:], v_early[:].indirect(listed(0, PASS)), ACT.Copy)
+        values[1, 1] = sb([P, PASS], BF16, "values11", after="neg_max10")
+        nc.vector.tensor_copy(values[1, 1][:, 0:QUARTER], v_pool[1][:].indirect(listed(PASS, PASS + QUARTER)))
 
         part = [sb([P, PASSES], F32, "part%d" % b) for b in range(QBLOCKS)]
-        p_sb = {}
-        w_codes = {}
-        w_sc = {}
+        prob = {}
         for b in range(QBLOCKS):
             for g in range(PASSES):
-                p_sb[b, g] = sb([P, PACK, P], F32, "p%d%d" % (b, g))
+                prob[b, g] = sb([P, PACK, P], F32, "prob%d%d" % (b, g), after="v_early" if b + g == 0 else "")
                 nc.scalar.activation(
-                    p_sb[b, g][:],
+                    prob[b, g][:],
                     neg_c[b, g][:],
                     ACT.Exp,
                     bias=neg_max[b, PASSES - 1][:],
                     scale=-1.0,
                     accum_out=part[b][:, g : g + 1],
                 )
+        nc.scalar.activation(values[1, 1][:, QUARTER:PASS], v_pool[1][:].indirect(listed(PASS + QUARTER, N)), ACT.Copy)
 
-        nc.scalar.activation(v_g[1, 1][:, PASS // 2 : PASS], v_pool[1][:].indirect(offsets[:, 48:64]), ACT.Copy)
-
+        values_bank = [banks[1], banks[2]]
+        v_bf = [sb([P, DV, PACK], BF16, "v_bf0", after="neg_max11"), sb([P, DV, PACK], BF16, "v_bf1")]
         v_codes = [sb([P, DV], U32, "v_codes%d" % g) for g in range(PASSES)]
-        v_sc = [sb([P, DV], U8, "v_sc%d" % g) for g in range(PASSES)]
-        v_bf = [sb([P, DV, PACK], BF16, "v_bf0", slot="neg_max11"), sb([P, DV, PACK], BF16, "v_bf1")]
-        w_bf = {}
+        v_scales = [sb([P, DV], U8, "v_scales%d" % g) for g in range(PASSES)]
 
         def turn_values(g):
-            bank = banks[(1, 2)[g]]
             for h in range(VBLOCKS):
-                pairs = v_g[h, g][:].bitcast(F32)
+                pairs = values[h, g][:].bitcast(F32)
                 for u in range(2):
-                    at = P * (2 * h + u)
-                    nc.tensor.transpose(bank[:, at : at + P], pairs[:, u : 2 * P : 2], ident[:])
+                    first = P * (2 * h + u)
+                    nc.tensor.transpose(values_bank[g][:, first : first + P], pairs[:, u : 2 * P : 2], ident[:])
 
         def lay_values(g):
-            bank = banks[(1, 2)[g]]
             nc.scalar.copy(
                 v_bf[g][:].rearrange("s e r -> s (e r)").bitcast(F32).rearrange("s (h f u) -> s h f u", h=VBLOCKS, u=2),
-                bank[:].rearrange("s (h u f) -> s h f u", h=VBLOCKS, u=2),
+                values_bank[g][:].rearrange("s (h u f) -> s h f u", h=VBLOCKS, u=2),
             )
 
-        def weights(b, g):
-            bank = banks[2 + 2 * b + g]
+        def quantise_values(g):
+            nc.vector.quantize_mx(v_codes[g][:].bitcast(FP8X4), v_scales[g][:], v_bf[g][:].rearrange("s e r -> s (e r)"))
+
+        w_bf = {}
+        w_codes = {}
+        w_scales = {}
+
+        def turn_weights(b, g):
             for r in range(PACK):
-                nc.tensor.transpose(bank[:, P * r : P * (r + 1)], p_sb[b, g][:, r, :], ident[:])
+                nc.tensor.transpose(banks[2 + 2 * b + g][:, P * r : P * (r + 1)], prob[b, g][:, r, :], ident[:])
+
+        def scale_weights(b, g):
             w_bf[b, g] = sb([P, P, PACK], BF16, "w_bf%d%d" % (b, g))
             nc.vector.tensor_tensor(
                 w_bf[b, g][:],
-                bank[:].rearrange("s (r q) -> s q r", r=PACK),
+                banks[2 + 2 * b + g][:].rearrange("s (r q) -> s q r", r=PACK),
                 vs_col[g][:].unsqueeze(1).to_broadcast([P, P, PACK]),
                 ALU.mult,
             )
 
         def quantise_weights(b, g):
             w_codes[b, g] = sb([P, P], U32, "w_codes%d%d" % (b, g))
-            w_sc[b, g] = sb([P, P], U8, "w_sc%d%d" % (b, g))
-            nc.vector.quantize_mx(w_codes[b, g][:].bitcast(FP8X4), w_sc[b, g][:], w_bf[b, g][:].rearrange("s q r -> s (q r)"))
-
-        def quantise_values(g):
-            nc.vector.quantize_mx(v_codes[g][:].bitcast(FP8X4), v_sc[g][:], v_bf[g][:].rearrange("s e r -> s (e r)"))
+            w_scales[b, g] = sb([P, P], U8, "w_scales%d%d" % (b, g))
+            nc.vector.quantize_mx(w_codes[b, g][:].bitcast(FP8X4), w_scales[b, g][:], w_bf[b, g][:].rearrange("s q r -> s (q r)"))
 
         turn_values(0)
-        weights(0, 0)
-        weights(0, 1)
+        for b in range(QBLOCKS):
+            for g in range(PASSES):
+                turn_weights(b, g)
+        scale_weights(0, 0)
+        scale_weights(0, 1)
         quantise_weights(0, 0)
-        weights(1, 0)
+        scale_weights(1, 0)
         quantise_weights(0, 1)
         lay_values(0)
         turn_values(1)
         lay_values(1)
-        weights(1, 1)
+        scale_weights(1, 1)
         quantise_values(0)
         quantise_weights(1, 0)
         quantise_values(1)
         quantise_weights(1, 1)
-        inv = []
+
+        inverse = []
         for b in range(QBLOCKS):
             total = sb([P, 1], F32, "total%d" % b)
             nc.gpsimd.tensor_tensor(total[:], part[b][:, 0:1], part[b][:, 1:2], ALU.add)
-            inv.append(sb([P, 1], F32, "inv%d" % b))
-            nc.vector.reciprocal(inv[b][:], total[:])
+            inverse.append(sb([P, 1], F32, "inverse%d" % b))
+            nc.vector.reciprocal(inverse[b][:], total[:])
 
+        out_bank = [banks[0], banks[7]]
         for g in range(PASSES):
             for b in range(QBLOCKS):
                 nc.tensor.matmul_mx(
-                    out=banks[6 + b][:, 0:DV],
+                    out=out_bank[b][:, 0:DV],
                     lhsT=w_codes[b, g][:].bitcast(FP8X4),
-                    lhsT_scale=w_sc[b, g][:],
+                    lhsT_scale=w_scales[b, g][:],
                     rhs=v_codes[g][:].bitcast(FP8X4),
-                    rhs_scale=v_sc[g][:],
+                    rhs_scale=v_scales[g][:],
                     start=(g == 0),
                     stop=(g == PASSES - 1),
                 )
         y = [sb([P, DV], F32, "y%d" % b) for b in range(QBLOCKS)]
-        nc.scalar.activation(y[0][:], banks[6][:, 0:DV], ACT.Copy, scale=inv[0][:])
-        nc.vector.tensor_scalar(y[1][:], banks[7][:, 0:DV], inv[1][:], None, ALU.mult)
+        nc.scalar.activation(y[0][:], out_bank[0][:, 0:DV], ACT.Copy, scale=inverse[0][:])
+        nc.vector.tensor_scalar(y[1][:], out_bank[1][:, 0:DV], inverse[1][:], None, ALU.mult)
         nc.scalar.dma_start(out[0, 0:P, :], y[0][:])
         nc.sync.dma_start(out[0, P : 2 * P, :], y[1][:])

@@ -54,13 +54,9 @@ def tile_attend_soft_cap_kb_srtq256n1024t2048_kernel(tc, qT, k_words, k_scales, 
         ks_words = ks_pool[:].bitcast(I32)
         nc.vector.memset(ks_words[:, 0 : T // 8], 0)
         nc.gpsimd.memset(ks_words[:, T // 8 : T // 4], 0)
-        seed = sb([P, 1], F32, "seed")
-        nc.vector.memset(seed[:], 0.0)
         make_identity(nc, ident[:])
         nc.vector.memset(kb_pool[0:LIVE, :].bitcast(I32), 0)
         nc.vector.memset(vs_pool[0:LIVE, :].bitcast(I32), 0)
-        warm = sb([P, 1], F32, "warm")
-        nc.scalar.activation(warm[:], seed[:], ACT.Tanh, bias=seed[:])
 
         nc.sync.dma_start(offsets[:], offs)
         nc.sync.dma_start(kb_pool[LIVE:P, :], kb[0:1, :])

from contextlib import ExitStack

import concourse.mybir as mybir
from concourse.masks import make_identity

N, T, D, DV, NQ = 1024, 2048, 512, 256, 256
CAP = 2.0
FLOPS = 2 * NQ * N * (D + DV)

F32 = mybir.dt.float32
BF16 = mybir.dt.bfloat16
I32 = mybir.dt.int32
U32 = mybir.dt.uint32
U16 = mybir.dt.uint16
U8 = mybir.dt.uint8
FP8X4 = mybir.dt.float8_e4m3fn_x4
ACT = mybir.ActivationFunctionType
ALU = mybir.AluOpType

P = 128
PACK = 4
PASS = P * PACK
PASSES = N // PASS
QBLOCKS = NQ // P
VBLOCKS = DV // P
LIVE = P - 1
QUARTER = N // 4
EARLY = T - N + PASS


def tile_attend_soft_cap_kb_srtq256n1024t2048_kernel(tc, qT, k_words, k_scales, vT, vs, kb, offs, out):
    nc = tc.nc
    with ExitStack() as ctx:
        keep = ctx.enter_context(tc.tile_pool(name="keep", bufs=1))
        psum = ctx.enter_context(tc.psum_pool(name="psum", bufs=1))
        banks = [psum.tile([P, PASS], F32, name="bank%d" % n) for n in range(8)]

        def sb(shape, dtype, name, after=""):
            return keep.tile(shape, dtype, name=name, tag=after or name, align_bytes=64)

        offsets = keep.tile([P, N // 16], U16, name="offsets")

        def listed(first, last):
            return offsets[:, first // 16 : last // 16]

        ks_pool = sb([P, T], U8, "ks_pool")
        kb_pool = sb([P, T], F32, "kb_pool")
        vs_pool = sb([P, T], F32, "vs_pool")
        kw_pool = sb([P, T], U32, "kw_pool")
        v_pool = [sb([P, T], F32, "v_pool%d" % h) for h in range(VBLOCKS)]
        q_raw = sb([P, PACK, NQ], F32, "q_raw")
        ident = sb([P, P], F32, "ident")

        ks_words = ks_pool[:].bitcast(I32)
        nc.vector.memset(ks_words[:, 0 : T // 8], 0)
        nc.gpsimd.memset(ks_words[:, T // 8 : T // 4], 0)
        make_identity(nc, ident[:])
        nc.vector.memset(kb_pool[0:LIVE, :].bitcast(I32), 0)
        nc.vector.memset(vs_pool[0:LIVE, :].bitcast(I32), 0)

        nc.sync.dma_start(offsets[:], offs)
        nc.sync.dma_start(kb_pool[LIVE:P, :], kb[0:1, :])
        nc.sync.dma_start(vs_pool[LIVE:P, :], vs[0:1, :])
        for quad in range(4):
            nc.sync.dma_start(
                ks_pool[32 * quad : 32 * quad + 4, :].bitcast(I32),
                k_scales[0, 4 * quad : 4 * quad + 4, :].bitcast(I32),
            )
        nc.sync.dma_start(q_raw[:], qT[0].rearrange("(p r) q -> p r q", r=PACK))
        nc.sync.dma_start(kw_pool[:].bitcast(I32), k_words[0].rearrange("p t r -> p (t r)").bitcast(I32))
        nc.sync.dma_start(v_pool[0][:], vT[0:P, :])
        v_early = sb([P, EARLY], F32, "v_early")
        nc.sync.dma_start(v_early[:], vT[P : 2 * P, 0:EARLY])
        nc.sync.dma_start(v_pool[1][:], vT[P : 2 * P, :])

        kb_row = sb([P, N], F32, "kb_row")
        nc.scalar.activation(kb_row[:], kb_pool[:].indirect(offsets[:]), ACT.Copy)
        key_words = [sb([P, QUARTER], U32, "key_words%d" % n) for n in range(N // QUARTER)]
        q_bf = sb([P, NQ, PACK], BF16, "q_bf")
        nc.scalar.copy(q_bf[:], q_raw[:].rearrange("p r q -> p q r"))
        vs_row = sb([P, N], F32, "vs_row", after="q_raw")
        nc.scalar.activation(vs_row[:], vs_pool[:].indirect(offsets[:]), ACT.Copy)
        key_scales = sb([P, N], U8, "key_scales")
        nc.vector.tensor_copy(key_scales[:], ks_pool[:].indirect(offsets[:]))
        q_codes = sb([P, NQ], U32, "q_codes")
        q_scales = sb([P, NQ], U8, "q_scales")
        nc.vector.quantize_mx(q_codes[:].bitcast(FP8X4), q_scales[:], q_bf[:].rearrange("p q r -> p (q r)"))

        half_bias = sb([P, PASSES, PACK], F32, "half_bias", after="vs_pool")
        for g in range(PASSES):
            for j in range(PACK):
                first = PASS * g + P * j
                nc.tensor.transpose(banks[g][:, P * j : P * (j + 1)], kb_row[:, first : first + P], ident[:])
            nc.scalar.activation(half_bias[:, g, :], banks[g][:, LIVE:PASS:P], ACT.Copy, scale=1.0 / CAP)

        for n in range(N // QUARTER):
            nc.vector.tensor_copy(key_words[n][:], kw_pool[:].indirect(listed(QUARTER * n, QUARTER * (n + 1))))

        vs_col = [sb([P, PACK], F32, "vs_col%d" % g) for g in range(PASSES)]
        for g in range(PASSES):
            nc.sync.dma_start(vs_col[g][:], vs_row[LIVE:P, PASS * g : PASS * (g + 1)].rearrange("o (s r) -> o s r", r=PACK))

        def score_tile(g, j):
            return banks[4 + 2 * g + j // 2][:, NQ * (j % 2) : NQ * (j % 2 + 1)]

        for g in range(PASSES):
            for j in range(PACK):
                first = PASS * g + P * j
                nc.tensor.matmul_mx(
                    out=score_tile(g, j),
                    lhsT=key_words[first // QUARTER][:, first % QUARTER : first % QUARTER + P].bitcast(FP8X4),
                    lhsT_scale=key_scales[:, first : first + P],
                    rhs=q_codes[:].bitcast(FP8X4),
                    rhs_scale=q_scales[:],
                    start=True,
                    stop=True,
                )
        tanh = {}
        for g in range(PASSES):
            for j in range(PACK):
                tanh[g, j] = sb([P, NQ], F32, "tanh%d%d" % (g, j))
                nc.scalar.activation(tanh[g, j][:], score_tile(g, j), ACT.Tanh, bias=half_bias[:, g, j : j + 1], scale=1.0 / CAP)

        values = {}
        for g in range(PASSES):
            values[0, g] = sb([P, PASS], BF16, "values0%d" % g)
            nc.vector.tensor_copy(values[0, g][:], v_pool[0][:].indirect(listed(PASS * g, PASS * (g + 1))))

        capped_bank = {(0, 0): banks[0], (0, 1): banks[1], (1, 0): banks[7], (1, 1): banks[6]}
        follows = {(0, 0): "v_pool0", (1, 0): "neg_max00"}
        neg_c = {}
        neg_max = {}
        for b in range(QBLOCKS):
            for g in range(PASSES):
                for j in range(PACK):
                    nc.tensor.transpose(capped_bank[b, g][:, P * j : P * (j + 1)], tanh[g, j][:, P * b : P * (b + 1)], ident[:])
            for g in range(PASSES):
                neg_c[b, g] = sb([P, PACK, P], F32, "neg_c%d%d" % (b, g), after=follows.get((b, g), ""))
                neg_max[b, g] = sb([P, 1], F32, "neg_max%d%d" % (b, g))
                nc.vector.tensor_scalar(
                    neg_c[b, g][:],
                    capped_bank[b, g][:].rearrange("q (s r) -> q r s", r=PACK),
                    -CAP,
                    neg_max[b, g - 1][:] if g > 0 else None,
                    ALU.mult,
                    ALU.min,
                    accum_out=neg_max[b, g][:],
                )

        values[1, 0] = sb([P, PASS], BF16, "values10", after="vs_pool")
        nc.scalar.activation(values[1, 0][:], v_early[:].indirect(listed(0, PASS)), ACT.Copy)
        values[1, 1] = sb([P, PASS], BF16, "values11", after="neg_max10")
        nc.vector.tensor_copy(values[1, 1][:, 0:QUARTER], v_pool[1][:].indirect(listed(PASS, PASS + QUARTER)))

        part = [sb([P, PASSES], F32, "part%d" % b) for b in range(QBLOCKS)]
        prob = {}
        for b in range(QBLOCKS):
            for g in range(PASSES):
                prob[b, g] = sb([P, PACK, P], F32, "prob%d%d" % (b, g), after="v_early" if b + g == 0 else "")
                nc.scalar.activation(
                    prob[b, g][:],
                    neg_c[b, g][:],
                    ACT.Exp,
                    bias=neg_max[b, PASSES - 1][:],
                    scale=-1.0,
                    accum_out=part[b][:, g : g + 1],
                )
        nc.scalar.activation(values[1, 1][:, QUARTER:PASS], v_pool[1][:].indirect(listed(PASS + QUARTER, N)), ACT.Copy)

        values_bank = [banks[1], banks[2]]
        v_bf = [sb([P, DV, PACK], BF16, "v_bf0", after="neg_max11"), sb([P, DV, PACK], BF16, "v_bf1")]
        v_codes = [sb([P, DV], U32, "v_codes%d" % g) for g in range(PASSES)]
        v_scales = [sb([P, DV], U8, "v_scales%d" % g) for g in range(PASSES)]

        def turn_values(g):
            for h in range(VBLOCKS):
                pairs = values[h, g][:].bitcast(F32)
                for u in range(2):
                    first = P * (2 * h + u)
                    nc.tensor.transpose(values_bank[g][:, first : first + P], pairs[:, u : 2 * P : 2], ident[:])

        def lay_values(g):
            nc.scalar.copy(
                v_bf[g][:].rearrange("s e r -> s (e r)").bitcast(F32).rearrange("s (h f u) -> s h f u", h=VBLOCKS, u=2),
                values_bank[g][:].rearrange("s (h u f) -> s h f u", h=VBLOCKS, u=2),
            )

        def quantise_values(g):
            nc.vector.quantize_mx(v_codes[g][:].bitcast(FP8X4), v_scales[g][:], v_bf[g][:].rearrange("s e r -> s (e r)"))

        w_bf = {}
        w_codes = {}
        w_scales = {}

        def turn_weights(b, g):
            for r in range(PACK):
                nc.tensor.transpose(banks[2 + 2 * b + g][:, P * r : P * (r + 1)], prob[b, g][:, r, :], ident[:])

        def scale_weights(b, g):
            w_bf[b, g] = sb([P, P, PACK], BF16, "w_bf%d%d" % (b, g))
            nc.vector.tensor_tensor(
                w_bf[b, g][:],
                banks[2 + 2 * b + g][:].rearrange("s (r q) -> s q r", r=PACK),
                vs_col[g][:].unsqueeze(1).to_broadcast([P, P, PACK]),
                ALU.mult,
            )

        def quantise_weights(b, g):
            w_codes[b, g] = sb([P, P], U32, "w_codes%d%d" % (b, g))
            w_scales[b, g] = sb([P, P], U8, "w_scales%d%d" % (b, g))
            nc.vector.quantize_mx(w_codes[b, g][:].bitcast(FP8X4), w_scales[b, g][:], w_bf[b, g][:].rearrange("s q r -> s (q r)"))

        turn_values(0)
        for b in range(QBLOCKS):
            for g in range(PASSES):
                turn_weights(b, g)
        scale_weights(0, 0)
        scale_weights(0, 1)
        quantise_weights(0, 0)
        scale_weights(1, 0)
        quantise_weights(0, 1)
        lay_values(0)
        turn_values(1)
        lay_values(1)
        scale_weights(1, 1)
        quantise_values(0)
        quantise_weights(1, 0)
        quantise_values(1)
        quantise_weights(1, 1)

        inverse = []
        for b in range(QBLOCKS):
            total = sb([P, 1], F32, "total%d" % b)
            nc.gpsimd.tensor_tensor(total[:], part[b][:, 0:1], part[b][:, 1:2], ALU.add)
            inverse.append(sb([P, 1], F32, "inverse%d" % b))
            nc.vector.reciprocal(inverse[b][:], total[:])

        out_bank = [banks[0], banks[7]]
        for g in range(PASSES):
            for b in range(QBLOCKS):
                nc.tensor.matmul_mx(
                    out=out_bank[b][:, 0:DV],
                    lhsT=w_codes[b, g][:].bitcast(FP8X4),
                    lhsT_scale=w_scales[b, g][:],
                    rhs=v_codes[g][:].bitcast(FP8X4),
                    rhs_scale=v_scales[g][:],
                    start=(g == 0),
                    stop=(g == PASSES - 1),
                )
        y = [sb([P, DV], F32, "y%d" % b) for b in range(QBLOCKS)]
        nc.scalar.activation(y[0][:], out_bank[0][:, 0:DV], ACT.Copy, scale=inverse[0][:])
        nc.vector.tensor_scalar(y[1][:], out_bank[1][:, 0:DV], inverse[1][:], None, ALU.mult)
        nc.scalar.dma_start(out[0, 0:P, :], y[0][:])
        nc.sync.dma_start(out[0, P : 2 * P, :], y[1][:])
